import numpy as np, ml_dtypes
CORES = [48,51,52,55]
N = 4
import mx_ref
BF = ml_dtypes.bfloat16
def gentries(a):
    return np.ascontiguousarray(a.reshape(8, 16, -1).transpose(0, 2, 1)).reshape(8, -1)
def gtable(e):
    e = np.asarray(e); return np.ascontiguousarray(e.reshape(8, -1, 16).transpose(0, 2, 1)).reshape(128, -1).astype(np.int32)
def gcols(t, e):
    v = np.concatenate([t.reshape(8, 16, -1, 4), np.zeros((8, 16, 1, 4), BF)], axis=2)
    return np.ascontiguousarray(np.stack([v[g][:, e[g]] for g in range(8)])).reshape(128, -1)
def tile(rs):
    return np.stack(rs, axis=2).reshape(128, -1).astype(BF)
def pick(q, e):
    c = np.concatenate([q[0].reshape(128, -1, 4), np.zeros((128, 1, 4), np.uint8)], axis=1); s = np.concatenate([q[1], np.ones((16, 1), np.uint8)], axis=1)
    return (np.ascontiguousarray(c[:, e].reshape(128, -1)), np.ascontiguousarray(s[:, e]))
def join(*qs):
    return (np.concatenate([q[0] for q in qs], axis=1), np.concatenate([q[1] for q in qs], axis=1))
def put(q, e, v):
    c, s = q[0].reshape(128, -1, 4).copy(), q[1].copy(); c[:, e] = v[0].reshape(128, -1, 4); s[:, e] = v[1]
    return (c.reshape(128, -1), s)
def pk(c, s):
    return (np.ascontiguousarray(c), mx_ref.live(s))
def emit(q):
    return q[0], q[1]
def packed(v, rng):
    q = [mx_ref.quantize(np.ascontiguousarray(v[r])) for r in range(N)]
    return np.stack([a for a, b in q]), np.stack([mx_ref.plane(b, rng) for a, b in q])
def values_of_codes():
    e, c = np.zeros((128, 128, 4), np.float32), np.zeros((128, 2, 4), np.uint8)
    e[np.arange(128), np.arange(128), 0] = 1
    c[:127, :, 0] = np.arange(256).reshape(2, 128).T[:127]
    return mx_ref.matmul(mx_ref.quantize(e.reshape(128, 512).astype(BF)), (c.reshape(128, 8), np.full((16, 2), 127, np.uint8))).T.reshape(-1).astype(np.float64)
CODE_VALUE, SCALE_VALUE = values_of_codes(), 2.0 ** (np.arange(256) - 127.0)
def decode(q):
    return (CODE_VALUE[q[0]].reshape(16, 8, -1, 4) * SCALE_VALUE[q[1]][:, None, :, None] + 0.0).reshape(128, -1).astype(np.float32)
def f(rng, *shape):
    return mx_ref.flush((rng.standard_normal(shape, dtype=np.float32) * np.exp2(rng.integers(-2, 3, shape[:-1] + (1,)))).astype(BF))
def wide(rng, *shape, cols=0):
    v = rng.standard_normal(shape, dtype=np.float32) * np.exp2(rng.integers(-12, 13, shape)).astype(np.float32)
    if cols: v *= np.repeat(np.exp2(rng.integers(-cols, cols + 1, shape[:-2] + (1, shape[-1] // 4))) * (rng.random(shape[:-2] + (1, shape[-1] // 4)) > 0.0625), 4, axis=-1).astype(np.float32)
    return mx_ref.flush(v.astype(BF))
C, STAGES = 480, 5
STEP = [1, 2, 3]
def numbers_of(rng):
    return {"x": np.array(f(rng, N, 128, 4 * C)), "u": np.array(f(rng, N, 128, 512)), "v": np.array(f(rng, N, 128, 512))}
def stored(a, b, s):
    return {"ta": np.stack([gtable(a[r]) for r in range(N)]), "tb": np.stack([gtable(b[r]) for r in range(N)]), "st": np.stack([gtable(s[r]) for r in range(N)])}
def lists(rng):
    e = np.tile(np.arange(C), (N, 8, 1))
    return stored(rng.permuted(e, axis=2), rng.permuted(e, axis=2), rng.permuted(e, axis=2))
def layers(rng):
    return np.array(f(rng, N, 128, 2048)).reshape(N, 8, 16, 4, 8, 16, 4)
def weights(rng, w):
    c, p = packed(np.ascontiguousarray(w).reshape(N, 128, 2048), rng)
    return {"wc": c, "ws": p}
def setup_inputs(rng):
    return {**numbers_of(rng), **lists(rng), **weights(rng, layers(rng))}
def setup_inputs_ties(rng):
    d = numbers_of(rng)
    o = rng.permutation(N)
    k = rng.integers(-1, 2, (2, N, 8, C)).astype(np.float32)
    k[0, o[1]] = 1
    x = d["x"].reshape(N, 8, 16, C, 4)
    x[:, :, [0, 1, 8]] = 0
    x[:, :, 0, :, 0] = k[0].astype(BF)
    x[:, :, 1, :, 0] = k[1].astype(BF)
    c = np.ones(N, np.float32)
    c[o[0]] = 0
    c[o[2]] = -1
    u = d["u"].reshape(N, 128, 128, 4)
    u[:, :, ::16] = 0
    for h in range(0, 128, 16):
        u[:, h, h, 0] = c.astype(BF)
        u[:, h + 8, h, 0] = c.astype(BF)
    w = layers(rng)
    w[:, :, :, :, :, [0, 1, 8]] = 0
    for g in range(8): w[:, g, 1, 0, g, 8, 0] = 32.0
    return {"x": x.reshape(N, 128, 4 * C), "u": u.reshape(N, 128, 512), "v": d["v"], **lists(rng), **weights(rng, w)}
def setup_inputs_near(rng):
    d = numbers_of(rng)
    o = rng.permutation(N) % 2
    k = np.where(o == 0, 2.0 ** -30, 1.0).astype(np.float32)
    x = np.zeros((N, 8, 16, C, 4), np.float32)
    s = rng.integers(-1, 2, (N, 8, C)) * k[:, None, None]
    x[:, :, 0, :, 0] = 1.125 * s
    x[:, :, 1, :, 0] = -1.25 * s
    for r in range(N):
        for g in rng.permutation(8)[:4]: x[r, g, 0, rng.integers(C), 0] = 2.0 ** 30 * rng.choice([-1.0, 1.0])
    x[:, :, 10, :, 0] = rng.integers(-1, 2, (N, 8, C)) * 2.0 ** -30
    x[:, :, 11, :, 0] = 2.0 ** -30
    u = d["u"].reshape(N, 128, 128, 4)
    u[:, :, ::16] = 0
    for h in range(0, 128, 16):
        u[:, h, h, 0] = (1.125 * k).astype(BF)
        u[:, h + 1, h, 0] = k.astype(BF)
        u[:, h + 8, h, 0] = k.astype(BF)
    w = np.zeros((N, 8, 16, 4, 8, 16, 4), np.float32)
    for g in range(8):
        w[:, g, 10, 0, g, 8, 0] = 2.0 ** -7
        w[:, g, 11, 0, g, 9, 0] = 2.0 ** 7
    for r in range(N):
        for g in rng.permutation(8)[:4]:
            w[r, g, 10, 0, g, 8, 0] = 2.0 ** -11
            w[r, g, 10, 0, g, 13, 0] = -2.0 ** -11
            w[r, g, 12, 0, g, 8, 0] = 2.0 ** -8
            w[r, g, 12, 0, g, 13, 0] = 2.0 ** -8
            w[r, g, 11, 0, g, 9, 0] = 2.0 ** 5
            u[r, 16 * g + 8, 16 * g, 0] = 1.125 * float(k[r])
            u[r, 16 * g + 13, 16 * g, 0] = float(k[r])
    return {"x": x.reshape(N, 128, 4 * C).astype(BF), "u": u.reshape(N, 128, 512), "v": d["v"], **lists(rng), **weights(rng, w.astype(BF))}
def setup_inputs_odd(rng):
    d = numbers_of(rng)
    x = (1.0 + (2 * rng.integers(0, 64, (N, 8, 16, C, 4)) + 1) * 2.0 ** -7) * np.exp2(-rng.integers(0, 7, (N, 8, 16, C, 4)).astype(np.float64)) * rng.choice([-1.0, 1.0], (N, 8, 16, C, 4))
    x[:, :, 0, :, 0] = 1.96875 * 2.0 ** 8 * rng.choice([-1.0, 1.0], (N, 8, C))
    x[:, :, 1:3] = 0
    x[:, :, 1, :, 0] = (8 + rng.integers(0, 2, (N, 8, C))) * 2.0 ** -8
    x[:, :, 2, :, 0] = -2.0 ** -5
    a = np.exp2(rng.integers(-3, 4, (N, 8, C)).astype(np.float64))
    x[:, :, 8:] = 0
    x[:, :, 8, :, 0] = 1.125 * a
    x[:, :, 11, :, 0] = (8 + rng.integers(0, 2, (N, 8, C))) * 2.0 ** -7 * a
    x[:, :, 12, :, 0] = 2.0 ** -4 * a
    u = d["u"].reshape(N, 128, 128, 4)
    u[:, :, ::16] = 0
    for h in range(0, 128, 16):
        for i in (1, 2, 9, 10): u[:, h + i, h, 0] = 1.0
    w = layers(rng)
    w[:, :, :3] = 0
    w[:, :, :, :, :, :3] = 0
    w[:, :, :, :, :, 8:] = 0
    for g in range(8):
        w[:, g, 8, 0, g, 8, 0] = 28.0
        w[:, g, 11, 0, g, 9, 0] = 2.0 ** -5
        w[:, g, 12, 0, g, 10, 0] = -2.0 ** -5
    return {"x": x.astype(np.float32).reshape(N, 128, 4 * C).astype(BF), "u": u.reshape(N, 128, 512), "v": d["v"], **lists(rng), **weights(rng, w)}
def setup_inputs_ends(rng):
    d = numbers_of(rng)
    o, e, h = rng.permutation(N) % 4, rng.permutation(N) % 4, rng.permutation(N) % 2
    s = rng.choice([-1.0, 1.0], (N, 8, 8, C, 4))
    s[o == 0] = -1
    s[o == 1] = rng.choice([-1.0, 1.0], (N, 1, 1, C, 1))[o == 1]
    low = s * (0.9 + 0.1 * rng.random((N, 8, 8, C, 4))) * 2.0 ** 30
    low[o == 3] = s[o == 3] * 2.0 ** -30
    x = d["x"].astype(np.float32).reshape(N, 8, 16, C, 4)
    x[:, :, :8] = low
    size = np.where(o == 3, 2.0 ** -30, 2.0 ** 30)
    c = np.stack([rng.permutation(8) % 2 * 2.0 - 1.0 for r in range(N)]) * size[:, None]
    u = d["u"].reshape(N, 128, 128, 4)
    u[:, :, ::16] = c.astype(np.float32).astype(BF)[:, None, :, None]
    v = rng.choice([-1.0, 1.0], (N, 128, 512)) * size[:, None, None]
    a, b, t = [rng.integers(0, C, (N, 8, C)) for i in range(3)]
    a[e == 0], b[e == 0], t[e == 0] = C - 1, C - 1, C - 1
    a[e == 1], b[e == 1], t[e == 1] = 0, C - 1, 0
    a[e == 2], b[e == 2], t[e == 2] = C - 1 - np.arange(C), np.arange(C), (np.arange(C) + 1) % 2 * (C - 1)
    w = np.zeros((N, 128, 4, 128, 4), np.float32)
    i = np.flatnonzero(np.arange(128) % 16 >= 8)
    for k in range(4): w[:, i, k, i, k] = np.where(h == 0, 2.0 ** 8, 2.0 ** -8)[:, None] * rng.choice([-1.0, 1.0], (N, 64))
    return {"x": x.reshape(N, 128, 4 * C).astype(BF), "u": u.reshape(N, 128, 512), "v": v.astype(np.float32).astype(BF), **stored(a, b, t), **weights(rng, w.astype(BF))}
def setup_inputs_spread(rng):
    d = setup_inputs(rng)
    d["x"] = wide(rng, N, 128, 4 * C, cols=6)
    return d
def check_inputs(d):
    b = []
    for k in ("x", "u", "v"):
        a = np.abs(d[k].astype(np.float32))
        if not (np.isfinite(a).all() and ((a == 0) | (a >= 2.0 ** -30) & (a <= 2.0 ** 30)).all()): b.append("a value of " + k)
    for k in ("ta", "tb", "st"):
        if not ((d[k] >= 0) & (d[k] < C)).all(): b.append("an entry of " + k)
    none, least, most = [emit(mx_ref.quantize(np.full((128, 16), k, np.float32).astype(BF)))[1][0, 0] for k in (0.0, 2.0 ** -8, 2.0 ** 8)]
    for r in range(N):
        if ((d["wc"][r] == 0x7F) | (d["wc"][r] == 0xFF)).any(): b.append("wc: a code that is no number")
        s = mx_ref.live(d["ws"][r])
        if ((s != none) & ((s < least) | (s > most))).any(): b.append("ws: a scale out of range")
    return b
def at(t, s):
    return np.take_along_axis(t, s, axis=2)
def reference(x, u, v, ta, tb, st, wc, ws):
    qu = [mx_ref.quantize(u[r]) for r in range(N)]
    lay = [pk(wc[r], ws[r]) for r in range(N)]
    a, b, s = [np.stack([gentries(k[r]) for r in range(N)]).astype(np.int64) for k in (ta, tb, st)]
    now = [x[r] for r in range(N)]
    for step in STEP:
        q = [mx_ref.quantize(now[r]) for r in range(N)]
        bit = np.stack([mx_ref.matmul(qu[r], q[r])[::16] > 0 for r in range(N)])
        for k in range(STAGES):
            right = np.roll(at(bit, s), -1, axis=2)
            s = np.where(right, at(b, s), at(a, s))
        z = [gcols(decode(q[r]).astype(BF), s[r]) for r in range(N)]
        qz = [mx_ref.quantize(z[r]) for r in range(N)]
        made, change = [], []
        for r in range(N):
            p = r ^ step
            h = tile([mx_ref.matmul(pick(lay[r], np.arange(128 * k, 128 * k + 128)), qz[p]) * np.float32(0.03125) for k in range(4)])
            change.append(mx_ref.matmul(qu[r], mx_ref.quantize(h))[::16] > 0)
            made.append((z[r].astype(np.float32) + gcols(h, s[p]).astype(np.float32)).astype(BF))
        c = np.stack(change)
        a, b = np.where(c, b, a), np.where(c, a, b)
        now = made
    y, op = np.zeros((N, 128, C), np.float32), np.zeros((N, 8, 3 * C), np.float32)
    oc, osc = np.zeros((N, 128, 4 * C), np.uint8), np.zeros((N, 16, C), np.uint8)
    for r in range(N):
        q = mx_ref.quantize(now[r])
        y[r] = mx_ref.matmul(mx_ref.quantize(v[r]), q)
        op[r] = np.concatenate([s[r], a[r], b[r]], axis=1)
        oc[r], osc[r] = emit(q)
    return {"y": y, "op": op, "oc": oc, "osc": osc}

from concourse.bass import DstId, RemoteDMATransfer
from concourse.mybir import dt, AluOpType, ActivationFunctionType

C = 480
L = 31
RUN = 16 * L
DUP = 2048
WIN = DUP + 2 * C
STEP = [1, 2, 3]
STAGES = 5

SCRATCH = {}


def _add(name, shape, dtype, where="sbuf"):
    SCRATCH[name] = (where, shape, dtype)


CODES = "float8_e4m3fn_x4"
for _n in ("xt",):
    _add(_n, [128, 4 * C], "bfloat16")
for _n in ("ut", "vt"):
    _add(_n, [128, 512], "bfloat16")
for _n in ("qu", "qr", "qv", "qe0", "qe1", "qe2", "qe3"):
    _add(_n, [128, 128], CODES)
    _add(_n + "s", [128, 128], "uint8")
_add("wq", [128, 512], CODES)
_add("wqs", [128, 512], "uint8")
for _r in range(4):
    _add("q%d" % _r, [128, C], CODES)
    _add("q%ds" % _r, [128, C], "uint8")
    _add("sl%d" % _r, [128, 32], "uint16")
for _r in range(3):
    _add("ql%d" % _r, [128, C], CODES)
    _add("ql%ds" % _r, [128, C], "uint8")
    _add("ll%d" % _r, [128, 32], "uint16")
for _n in ("qz", "qh"):
    _add(_n, [128, C], CODES)
    _add(_n + "s", [128, C], "uint8")
for _n in ("X", "Zp", "H"):
    _add(_n, [128, 4 * C], "bfloat16")
for _b in range(4):
    _add("to%d" % _b, [128, C], "bfloat16")
    _add("tp%d" % _b, [128, C], "bfloat16")
    _add("zo%d" % _b, [128, C], "bfloat16")
for _n in ("hw0", "hw1", "sg", "xs", "d0h"):
    _add(_n, [128, C], "bfloat16")
for _n in ("raw", "words"):
    _add(_n, [128, WIN], "float32")
for _n in ("t", "i2"):
    _add(_n, [128, C], "float32")
_add("G", [128, RUN + 16], "float32")
_add("St", [128, RUN], "float32")
_add("d0", [128, RUN], "float32")
_add("one", [128, 528], "bfloat16")
_add("eye", [128, 528], "bfloat16")
for _n in ("wt", "sm", "s2", "bt", "mv", "laf", "lbf", "df"):
    _add(_n, [128, 32], "float32")
for _n in ("o", "la", "lb", "l2", "l3"):
    _add(_n, [128, 32], "uint16")
for _n in ("sti", "tai", "tbi"):
    _add(_n, [128, 30], "int32")
_add("di", [128, 16], "int32")
_add("dm", [128, 16], "int32")
_add("qi", [128, 8], "int32")
_add("qm", [128, 8], "int32")
_add("ip", [128, 8], "int32")
_add("ip16", [128, 8], "uint16")
_add("ma", [128, 16], "float32")
_add("mb", [128, 16], "float32")
_add("mc", [128, 16], "float32")
for _n in ("ka", "kb", "kc", "kd", "ke", "sc", "sch", "si", "wp"):
    _add(_n, [128, 8], "float32")
_add("yb", [128, C], "float32")
_add("opb", [128, 3 * C], "float32")
for _b in range(8):
    _add("ps%d" % _b, [128, 512], "float32", "psum")

LOADS = ["x", "u", "st", "ta", "tb", "wc", "ws", "v"]
SEMAPHORES = ["cv", "ca", "cp", "cg", "out", "left"] + ["ld_" + n for n in LOADS]
SEMAPHORES += ["rq%d" % r for r in range(3)] + ["rl%d" % r for r in range(3)]


def rank_program(g, core, T, topo):
    rank = T.rank_of(core)
    if rank is None:
        return
    A = AluOpType
    COPY = ActivationFunctionType.Copy
    SIGN = ActivationFunctionType.Sign
    eng = {"v": g.vector, "a": g.scalar, "p": g.tensor, "g": g, "s": g.sync}
    total = {}
    know = {q: {} for q in eng}
    wrote = {}
    read = {}

    def wait(q, toks):
        toks = [t for t in toks if know[q].get(t[1], 0) < t[2]]
        keep = []
        for i, t in enumerate(toks):
            if not any(j != i and o[3].get(t[1], 0) >= t[2] and (o[1:3] != t[1:3] or j < i) for j, o in enumerate(toks)):
                keep.append(t)
        for t in keep:
            eng[q].wait_ge(T.sem[t[1]], t[2])
            for s, n in t[3].items():
                know[q][s] = max(know[q].get(s, 0), n)

    def before(q, reads, writes, banks):
        toks = [wrote[k] for k in reads if k in wrote]
        for k in list(writes) + list(banks):
            if k in wrote and (wrote[k][0] != q):
                toks.append(wrote[k])
            toks += [t for t in read.get(k, {}).values() if t[0] != q]
        wait(q, toks)

    def after(q, sem, n, reads, writes, banks):
        total[sem] = total.get(sem, 0) + n
        clk = dict(know[q])
        clk[sem] = total[sem]
        tok = (q, sem, total[sem], clk)
        for k in reads:
            read.setdefault(k, {})[q] = tok
        for k in list(writes) + list(banks):
            wrote[k] = tok
            read[k] = {}
        return tok

    def op(q, call, reads, writes, banks=()):
        before(q, reads, writes, banks)
        call().then_inc(T.sem["c" + q], 1)
        return after(q, "c" + q, 1, reads, writes, banks)

    def dma(q, out, in_, sem, reads=(), writes=()):
        before(q, reads, writes, ())
        eng[q].dma_start(out, in_).then_inc(T.sem[sem], 16)
        return after(q + "dma" + sem, sem, 16, reads, writes, ()) if False else _dma_after(q, sem, reads, writes)

    def _dma_after(q, sem, reads, writes):
        total[sem] = total.get(sem, 0) + 16
        clk = dict(know[q])
        clk[sem] = total[sem]
        tok = ("dma", sem, total[sem], clk)
        for k in reads:
            read.setdefault(k, {})["dma" + sem] = tok
        for k in writes:
            wrote[k] = tok
            read[k] = {}
        return tok

    def vcopy(out, in_, reads, writes, banks=()):
        return op("v", lambda: g.vector.tensor_copy(out, in_), reads, writes, banks)

    def vts(out, in_, s1, s2, op0, op1, reads, writes, banks=()):
        if op1 is None:
            return op("v", lambda: g.vector.tensor_scalar(out, in_, s1, None, op0), reads, writes, banks)
        return op("v", lambda: g.vector.tensor_scalar(out, in_, s1, s2, op0, op1), reads, writes, banks)

    def vtt(out, a, b, o, reads, writes, banks=()):
        return op("v", lambda: g.vector.tensor_tensor(out, a, b, o), reads, writes, banks)

    def vset(ap, c, writes):
        return op("v", lambda: g.vector.memset(ap, c), [], writes)

    def act(out, in_, reads, writes, banks=(), func=COPY, scale=1.0):
        if scale == 1.0:
            return op("a", lambda: g.scalar.activation(out, in_, func), reads, writes, banks)
        return op("a", lambda: g.scalar.activation(out, in_, func, scale=scale), reads, writes, banks)

    def quant(name, tile_ap, reads):
        return op("v", lambda: g.vector.quantize_mx(T[name][:], T[name + "s"][:], tile_ap), reads, [name])

    def mx(bank, w, wcols, x, xcols):
        n = xcols[1] - xcols[0]
        return op("p", lambda: g.tensor.matmul_mx(T["ps%d" % bank][:, 0:n], T[w][:, wcols[0]:wcols[1]], T[w + "s"][:, wcols[0]:wcols[1]],
                                                   T[x][:, xcols[0]:xcols[1]], T[x + "s"][:, xcols[0]:xcols[1]], True, True),
                  [w, x], [], ["ps%d" % bank])

    ALL = (0, C)
    W0 = (0, 128)
    ps = lambda b: T["ps%d" % b][:, 0:C]
    bank = lambda b: ["ps%d" % b]
    ends = T.St[:, 15:RUN:16]

    dma("s", T.xt[:], T.x[:], "ld_x", writes=["xt"])
    dma("a", T.ut[:], T.u[:], "ld_u", writes=["ut"])
    dma("a", T.sti[:], T.st[:], "ld_st", writes=["sti"])
    dma("a", T.tai[:], T.ta[:], "ld_ta", writes=["tai"])
    dma("a", T.tbi[:], T.tb[:], "ld_tb", writes=["tbi"])
    dma("s", T.wq[:].bitcast(dt.uint8), T.wc[:], "ld_wc", writes=["wq"])
    dma("s", T.wqs[:], T.ws[:], "ld_ws", writes=["wqs"])
    dma("s", T.vt[:], T.v[:], "ld_v", writes=["vt"])

    vset(T.one[:], 1.0, ["one"])
    op("g", lambda: g.iota(T.ip[:], [[16, 8]], 0, 0), [], ["ip"])
    op("g", lambda: g.iota(T.qi[:], [[0, 8]], 0, 1), [], ["qi"])
    op("g", lambda: g.iota(T.di[:], [[1, 16]], 128, -1), [], ["di"])
    op("g", lambda: g.iota(T.i2[:], [[2, C]], 0, 0, allow_small_or_imprecise_dtypes=True), [], ["i2"])
    op("g", lambda: g.affine_select(T.eye[:], T.one[:], [[-1, 528]], A.is_equal, 0.0, 3, 4), ["one"], ["eye"])
    vset(T.raw[:, 2 * C:DUP], 0.0, ["rawgap"])
    vset(T.words[:, 2 * C:DUP], 0.0, ["wordgap"])
    vset(T.G[:, RUN:RUN + 16], 0.0, ["Gtail"])
    vcopy(T.ip16[:], T.ip[:], ["ip"], ["ip16"])
    c1 = slice(0, 1)
    vts(T.qm[:], T.qi[:], 15, None, A.bitwise_and, None, ["qi"], ["qm"])
    vts(T.dm[:], T.di[:], 15, None, A.bitwise_and, None, ["di"], ["dm"])
    vts(T.ka[:], T.qm[:], 13, 2.0 ** -27, A.is_le, A.mult, ["qm"], ["ka"])
    vts(T.kb[:], T.qm[:], 14, 2.0 ** -11, A.is_equal, A.mult, ["qm"], ["kb"])
    vts(T.kc[:], T.qm[:], 15, 1.0, A.is_equal, A.mult, ["qm"], ["kc"])
    vts(T.kd[:], T.qm[:], 13, 2.0 ** 28, A.is_le, A.mult, ["qm"], ["kd"])
    vts(T.ke[:], T.qm[:], 14, 2.0 ** 12, A.is_equal, A.mult, ["qm"], ["ke"])
    vts(T.wp[:], T.qm[:], 15, 2.0 ** -11, A.is_equal, A.mult, ["qm"], ["wp"])
    vts(T.ma[:], T.dm[:], 1, 2047.0, A.is_equal, A.mult, ["dm"], ["ma"])
    vts(T.mb[:], T.dm[:], 2, 65535.0, A.is_equal, A.mult, ["dm"], ["mb"])
    vts(T.mc[:], T.dm[:], 0, 1.0, A.not_equal, A.mult, ["dm"], ["mc"])
    vtt(T.ka[:], T.ka[:], T.kb[:], A.add, ["ka", "kb"], ["ka"])
    vtt(T.kd[:], T.kd[:], T.ke[:], A.add, ["kd", "ke"], ["kd"])
    vts(T.ke[:], T.kc[:], 2.0, None, A.mult, None, ["kc", "kd"], ["ke"])
    vtt(T.ma[:], T.ma[:], T.mb[:], A.add, ["ma", "mb"], ["ma"])
    vtt(T.sc[:], T.ka[:], T.kc[:], A.add, ["ka", "kc"], ["sc"])
    vtt(T.si[:], T.kd[:], T.ke[:], A.add, ["kd", "ke"], ["si"])
    vtt(T.d0[:, 0:16], T.ma[:], T.mc[:], A.add, ["ma", "mc"], ["d0"])
    vts(T.sch[:], T.sc[:], 0.5, None, A.mult, None, ["sc"], ["sch"])
    vcopy(T.la[:, 0:30], T.tai[:], ["tai"], ["la"])
    vcopy(T.lb[:, 0:30], T.tbi[:], ["tbi"], ["lb"])
    vcopy(T.sl0[:, 0:30], T.sti[:], ["sti"], ["sl0"])
    vcopy(T.sl0[:, 30:31], T.sti[:, 0:1], ["sti"], ["sl0"])
    n = 16
    while n < RUN:
        m = min(n, RUN - n)
        vcopy(T.d0[:, n:n + m], T.d0[:, 0:m], ["d0"], ["d0"])
        n += m
    quant("qu", T.ut[:], ["ut"])
    quant_pick = T.qu[:, 0:128].bitcast(dt.uint32).indirect(T.ip16[:, 0:8])
    vcopy(T.qr[:, 0:128].bitcast(dt.uint32), quant_pick, ["qu", "ip16"], ["qr"])
    vcopy(T.qrs[:, 0:128], T.qus[:, 0:128].indirect(T.ip16[:, 0:8]), ["qu", "ip16"], ["qrs"])
    quant("q0", T.xt[:], ["xt"])
    for b in range(4):
        quant("qe%d" % b, T.eye[:, 3 - b:515 - b], ["eye"])
    vcopy(T.d0h[:], T.d0[:, 0:C], ["d0"], ["d0h"])
    vts(T.s2[:, 0:L], T.sl0[:, 0:L], T.si[:, c1], None, A.mult, None, ["sl0", "si"], ["s2"])
    vcopy(T.laf[:, 0:30], T.tai[:], ["tai"], ["laf"])
    vcopy(T.lbf[:, 0:30], T.tbi[:], ["tbi"], ["lbf"])
    vtt(T.df[:, 0:30], T.lbf[:, 0:30], T.laf[:, 0:30], A.subtract, ["laf", "lbf"], ["df"])

    def tables():
        act(T.raw[:, 0:2 * C:2], T.i2[:, 0:C].indirect(T.la[:, 0:30]), ["i2", "la"], ["raw0"])
        act(T.raw[:, 1:2 * C:2], T.i2[:, 0:C].indirect(T.lb[:, 0:30]), ["i2", "lb"], ["raw1"])

    def scan():
        return op("v", lambda: g.vector.tensor_tensor_scan(T.St[:], T.d0[:], T.G[:, 0:RUN], 0.0, A.mult, A.add), ["d0", "G"], ["St"])

    def send(r, dst, name, land, cols, sem, reads, codes=False):
        rid, pid = topo.addr(dst)[:2]
        mask = topo.mask(core, dst)
        before("g", reads, [], [])
        n = len(topo.engines(core, dst))
        src, out = T[name][:, 0:cols], T[land][:, 0:cols]
        if codes:
            src, out = src.bitcast(dt.uint8), out.bitcast(dt.uint8)
        g.remote_dma(out, src, T.sem[sem], T.sem.left, pid, rid, mask)
        total["left"] = total.get("left", 0) + n
        total[sem] = total.get(sem, 0) + n

    def arrives(keys, sem):
        for k in keys:
            wrote[k] = ("far", sem, total[sem], {sem: total[sem]})

    for r, step in enumerate(STEP):
        last = r == len(STEP) - 1
        dst = T.cores[rank ^ step]
        q, ql, ll, sl, sn = "q%d" % r, "ql%d" % r, "ll%d" % r, "sl%d" % r, "sl%d" % (r + 1)
        send(r, dst, q, ql, C, "rq%d" % r, [q], codes=True)
        send(r, dst, q + "s", ql + "s", C, "rq%d" % r, [q])
        arrives([ql], "rq%d" % r)
        op("p", lambda: g.tensor.matmul_mx(ps(0), T.qr[:], T.qrs[:], T[q][:], T[q + "s"][:], True, True), ["qr", "qrs", q], [], bank(0))
        tables()
        vts(T.t[:], ps(0), 0.0, float(DUP), A.is_gt, A.mult, [], ["t"], bank(0)) if False else None
        op("v", lambda: g.vector.tensor_scalar(T.t[:], ps(0), 0.0, float(DUP), A.is_gt, A.mult), ["ps0"], ["t"], bank(0))
        act(T.G[:, 0:RUN], T.t[:, 0:C].indirect(T[sl][:, 0:L]), ["t", sl], ["G"])
        for h, ls in ((0, "la"), (1, "lb")):
            vtt(T.words[:, h:2 * C:2], T.t[:, 0:C].indirect(T[ls][:, 0:30]), T.raw[:, h:2 * C:2], A.add, ["t", ls, "raw%d" % h], ["words%d" % h])
            act(T.words[:, DUP + h:WIN:2], T.words[:, h:2 * C:2], ["words%d" % h], ["dup%d" % h])
        act(T.raw[:, DUP:WIN], T.raw[:, 0:2 * C], ["raw0", "raw1"], ["rawdup"])
        for b in range(4):
            mx(2 + b, "qe%d" % b, W0, q, ALL)
            act(T["to%d" % b][:], ps(2 + b), ["ps%d" % (2 + b)], ["to%d" % b], bank(2 + b))
        for b, k in enumerate((6, 7, 2, 3)):
            mx(k, "qe%d" % b, W0, ql, ALL)
            act(T["tp%d" % b][:], ps(k), ["ps%d" % k], ["tp%d" % b], bank(k))
        for k in range(STAGES):
            if k:
                op("v", lambda: g.vector.tensor_copy(T.G[:, 0:RUN], T.words[:, 0:WIN].indirect(T.o[:, 0:L])),
                   ["o", "words0", "words1", "dup0", "dup1", "wordgap"], ["G"])
            scan()
            vts(T.wt[:, 0:L], T.G[:, 16:RUN + 16:16], T.wp[:, c1], None, A.mult, None, ["G", "Gtail", "wp"], ["wt"])
            if k == 0:
                vtt(T.wt[:, 0:L], T.wt[:, 0:L], T.s2[:, 0:L], A.add, ["wt", "s2"], ["wt"])
            vtt(T.sm[:, 0:L], ends, T.wt[:, 0:L], A.add, ["St", "wt"], ["sm"])
            vts(T.o[:, 0:L], T.sm[:, 0:L], T.sc[:, c1], 0.015625, A.mult, A.add, ["sm", "sc"], ["o"])
        vcopy(T.G[:, 0:RUN], T.raw[:, 0:WIN].indirect(T.o[:, 0:L]), ["o", "raw0", "raw1", "rawdup", "rawgap"], ["G"])
        scan()
        vts(T[sn][:, 0:L], ends, T.sch[:, c1], 0.015625, A.mult, A.add, ["St", "sch"], [sn])
        send(r, dst, sn, ll, 30, "rl%d" % r, [sn])
        arrives([ll], "rl%d" % r)
        own = T[sn][:, 0:30]
        for b in (0, 1):
            act(T["zo%d" % b][:], T["to%d" % b][:, 0:C].indirect(own), ["to%d" % b, sn], ["zo%d" % b])
        for b in (2, 3):
            vcopy(T["zo%d" % b][:], T["to%d" % b][:, 0:C].indirect(own), ["to%d" % b, sn], ["zo%d" % b])
        if not last:
            vts(T.s2[:, 0:L], T[sn][:, 0:L], T.si[:, c1], None, A.mult, None, [sn, "si"], ["s2"])
        if r == 0:
            quant("qv", T.vt[:], ["vt"])
        if last:
            vts(T.opb[:, 0:C], T.G[:, 0:C], 0.5, None, A.mult, None, ["G"], ["op0"])
        far = T[ll][:, 0:30]
        for b in (0, 1):
            act(T.Zp[:, b:4 * C:4], T["tp%d" % b][:, 0:C].indirect(far), ["tp%d" % b, ll], ["Zp%d" % b])
        for b in (2, 3):
            vcopy(T.Zp[:, b:4 * C:4], T["tp%d" % b][:, 0:C].indirect(far), ["tp%d" % b, ll], ["Zp%d" % b])
        quant("qz", T.Zp[:], ["Zp%d" % b for b in range(4)])
        for b in (2, 3):
            vts(T["l%d" % b][:, 0:30], far, 4, b, A.mult, A.add, [ll], ["l%d" % b])
        for b in range(4):
            op("p", lambda: g.tensor.matmul_mx(ps(4 + b), T.wq[:, 128 * b:128 * b + 128], T.wqs[:, 128 * b:128 * b + 128], T.qz[:], T.qzs[:], True, True),
               ["wq", "wqs", "qz"], [], bank(4 + b))
            if b < 2:
                act(T["hw%d" % b][:], ps(4 + b), ["ps%d" % (4 + b)], ["hw%d" % b], bank(4 + b), scale=0.03125)
            else:
                act(T.H[:, b:4 * C:4], ps(4 + b), ["ps%d" % (4 + b)], ["H%d" % b], bank(4 + b), scale=0.03125)
        for b in (0, 1):
            vtt(T.X[:, b:4 * C:4], T["hw%d" % b][:, 0:C].indirect(far), T["zo%d" % b][:], A.add, ["hw%d" % b, ll, "zo%d" % b], ["X%d" % b])
        for b in (0, 1):
            vcopy(T.H[:, b:4 * C:4], T["hw%d" % b][:], ["hw%d" % b], ["H%d" % b])
        HS = ["H%d" % b for b in range(4)]
        quant("qh", T.H[:], HS)
        op("p", lambda: g.tensor.matmul_mx(ps(1), T.qr[:], T.qrs[:], T.qh[:], T.qhs[:], True, True), ["qr", "qrs", "qh"], [], bank(1))
        act(T.sg[:], ps(1), ["ps1"], ["sg"], bank(1), func=SIGN)
        for b in (2, 3):
            vtt(T.X[:, b:4 * C:4], T.H[:, 0:4 * C].indirect(T["l%d" % b][:, 0:30]), T["zo%d" % b][:], A.add, HS + ["l%d" % b, "zo%d" % b], ["X%d" % b])
        quant("q%d" % (r + 1), T.X[:], ["X%d" % b for b in range(4)])
        op("v", lambda: g.vector.tensor_tensor_scan(T.xs[:], T.d0h[:], T.sg[:], 0.0, A.mult, A.add), ["d0h", "sg"], ["xs"])
        vts(T.bt[:, 0:30], T.xs[:, 15:C:16], T.sc[:, c1], 0.5, A.mult, A.is_gt, ["xs", "sc"], ["bt"])
        vtt(T.mv[:, 0:30], T.bt[:, 0:30], T.df[:, 0:30], A.mult, ["bt", "df"], ["mv"])
        vtt(T.laf[:, 0:30], T.laf[:, 0:30], T.mv[:, 0:30], A.add, ["laf", "mv"], ["laf"])
        vtt(T.lbf[:, 0:30], T.lbf[:, 0:30], T.mv[:, 0:30], A.subtract, ["lbf", "mv"], ["lbf"])
        vcopy(T.la[:, 0:30], T.laf[:, 0:30], ["laf"], ["la"])
        vcopy(T.lb[:, 0:30], T.lbf[:, 0:30], ["lbf"], ["lb"])
        if not last:
            vtt(T.df[:, 0:30], T.lbf[:, 0:30], T.laf[:, 0:30], A.subtract, ["laf", "lbf"], ["df"])

    dma("s", T.oc[:], T.q3[:].bitcast(dt.uint8), "out", reads=["q3"])
    for k in range(4):
        dma("s", T.osc[4 * k:4 * k + 4, :], T.q3s[32 * k:32 * k + 4, :], "out", reads=["q3"])
    half = C // 2
    mx(0, "qv", W0, "q3", (0, half))
    mx(2, "qv", W0, "q3", (half, C))
    op("a", lambda: g.scalar.activation(T.yb[:, 0:half], T.ps0[:, 0:half], COPY), ["ps0"], ["y0"], bank(0))
    dma("s", T.y[:, 0:half], T.yb[:, 0:half], "out", reads=["y0"])
    op("v", lambda: g.vector.tensor_copy(T.yb[:, half:C], T.ps2[:, 0:half]), ["ps2"], ["y1"], bank(2))
    dma("s", T.y[:, half:C], T.yb[:, half:C], "out", reads=["y1"])
    act(T.opb[:, C:2 * C], T.i2[:, 0:C].indirect(T.la[:, 0:30]), ["i2", "la"], ["op1"], scale=0.5)
    vts(T.opb[:, 2 * C:3 * C], T.i2[:, 0:C].indirect(T.lb[:, 0:30]), 0.5, None, A.mult, None, ["i2", "lb"], ["op2"])
    dma("s", T.op[:], T.opb[0:128:16, :], "out", reads=["op0", "op1", "op2"])
    for s in sorted(total):
        if know["g"].get(s, 0) < total[s]:
            g.wait_ge(T.sem[s], total[s])
